import numpy as np
import ml_dtypes


def mxq(x, axis, fmt="e4m3"):
    dtype, down = {"e4m3": (ml_dtypes.float8_e4m3fn, 7), "e5m2": (ml_dtypes.float8_e5m2, 14)}[fmt]
    v = np.moveaxis(np.asarray(x, np.float32).astype(ml_dtypes.bfloat16).astype(np.float64), axis, -1)
    blocks = v.reshape(v.shape[:-1] + (-1, 32))
    amax = np.abs(blocks).max(-1, keepdims=True)
    byte = np.maximum(np.where(amax > 0, np.frexp(amax)[1] - 1 + 127, 0) - down, 1)
    scale = np.exp2(byte - 127.0)
    codes = (blocks / scale).astype(np.float32).astype(dtype).astype(np.float64)
    return np.moveaxis((codes * scale).reshape(v.shape), -1, axis)


WIDE = False


def mx_kscale(k, group=512):
    if not WIDE:
        return np.ones(k)
    levels = np.array([18, -18])
    if group != 512:
        return np.exp2(np.random.permutation(np.resize(levels, k // group))).repeat(group)
    if k % 512:
        return np.exp2(np.random.permutation(np.resize(levels, k // 32))).repeat(32)
    a = np.empty((k // 512, 16))
    for p in range(k // 512):
        a[p, :8] = np.random.permutation(np.resize(levels, 8))
        for g in range(8):
            far = levels[np.abs(levels - a[p, g]) >= 10]
            a[p, g + 8] = far[np.random.randint(len(far))]
    return np.exp2(a.ravel()).repeat(32)


def f64(x):
    return np.asarray(x).astype(np.float64)


def sigmoid(v):
    return 1.0 / (1.0 + np.exp(-v))


G, D, M, N = 4, 128, 128, 512


def setup_inputs():
    n = np.random.standard_normal
    s_d = mx_kscale(D, 0)
    return {
        "h": (n((G, D, N)) * s_d[:, None]).astype(np.float32),
        "wr": (n((G, D, M)) / np.sqrt(D) / s_d[:, None]).astype(np.float32),
        "wu": (n((G, D, M)) / np.sqrt(D) / s_d[:, None]).astype(np.float32),
        "wc": (n((G, D, M)) / np.sqrt(D) / s_d[:, None]).astype(np.float32),
        "xr": (n((G, M, N))).astype(np.float32),
        "xu": (n((G, M, N))).astype(np.float32),
        "xc": (n((G, M, N))).astype(np.float32),
        "hp": (n((G, M, N))).astype(np.float32),
        "bc": (0.5 * n((G, M, 1))).astype(np.float32),
    }


def reference(h, wr, wu, wc, xr, xu, xc, hp, bc):
    wrq = mxq(f64(wr), 1, "e4m3")
    hq = mxq(f64(h), 1, "e4m3")
    zr = wrq.transpose(0, 2, 1) @ hq
    wuq = mxq(f64(wu), 1, "e4m3")
    zu = wuq.transpose(0, 2, 1) @ hq
    wcq = mxq(f64(wc), 1, "e4m3")
    zc = wcq.transpose(0, 2, 1) @ hq
    u = sigmoid(zu + f64(xu))
    cd = np.tanh(f64(xc) + sigmoid(zr + f64(xr)) * (zc + f64(bc)))
    y = (1.0 - u) * cd + u * f64(hp)
    return y

@@ -1,0 +1,269 @@
+from contextlib import ExitStack
+
+import concourse.mybir as mybir
+
+G, D, M, N = 4, 128, 128, 512
+FLOPS = 3 * 2 * G * D * M * N
+
+F32 = mybir.dt.float32
+BF16 = mybir.dt.bfloat16
+U32 = mybir.dt.uint32
+U8 = mybir.dt.uint8
+FP8X4 = mybir.dt.float8_e4m3fn_x4
+ALU = mybir.AluOpType
+ACT = mybir.ActivationFunctionType
+
+P = 128
+PACK = 4
+ROWS = D // PACK
+HALF = N // 2
+PIECES = [(0, 256), (256, 384), (384, 512)]
+N_MM = 128
+ALL, LO, HI = slice(0, N), slice(0, HALF), slice(HALF, N)
+
+
+def tile_rows_cell_gru_kernel(tc, h, wr, wu, wc, xr, xu, xc, hp, bc, out):
+    nc = tc.nc
+    with ExitStack() as ctx:
+        sb = ctx.enter_context(tc.tile_pool(name="sb", bufs=1))
+        ps = ctx.enter_context(tc.psum_pool(name="ps", bufs=1))
+        ctx.enter_context(tc.manual_schedule())
+
+        def per_head(name):
+            return [sb.tile([P, N], F32, name="%s%d" % (name, g)) for g in range(G)]
+
+        weights = {"r": wr, "u": wu, "c": wc}
+        w_raw, w_bf, w_codes, w_scales = {}, {}, {}, {}
+        for k in weights:
+            w_raw[k] = sb.tile([P, PACK, M], F32, name="w_raw_" + k)
+            w_bf[k] = sb.tile([P, M, PACK], BF16, name="w_bf_" + k, align_bytes=64)
+            w_codes[k] = sb.tile([P, M], U32, name="w_codes_" + k, align_bytes=64)
+            w_scales[k] = sb.tile([P, M], U8, name="w_scales_" + k, align_bytes=64)
+        h_raw = [sb.tile([P, PACK, b - a], F32, name="h_raw%d" % a) for a, b in PIECES]
+        h_bf = [sb.tile([P, b - a, PACK], BF16, name="h_bf%d" % a, align_bytes=64) for a, b in PIECES]
+        h_codes = sb.tile([P, N], U32, align_bytes=64)
+        h_scales = sb.tile([P, N], U8, align_bytes=64)
+        bias = sb.tile([P, G, 8], F32)
+
+        xr_sb, xu_sb, xc_sb, hp_sb = per_head("xr"), per_head("xu"), per_head("xc"), per_head("hp")
+        pre_r, gate_r = per_head("pre_r"), per_head("gate_r")
+        pre_u, gate_u = per_head("pre_u"), per_head("gate_u")
+        gated, pre_c, cand = per_head("gated"), per_head("pre_c"), per_head("cand")
+        kept, fresh, y = per_head("kept"), per_head("fresh"), per_head("y")
+        bank_ru = [ps.tile([M, N], F32, name="bank_ru%d" % g) for g in range(G)]
+        bank_c = [ps.tile([M, N], F32, name="bank_c%d" % g) for g in range(G)]
+
+        h_view = h.rearrange("g (p j) n -> (g p) j n", j=PACK)
+
+        def load_w(k):
+            nc.sync.dma_start(out=w_raw[k][:], in_=weights[k].rearrange("g (p j) m -> (g p) j m", j=PACK))
+
+        def load_h(i):
+            nc.sync.dma_start(out=h_raw[i][:], in_=h_view[:, :, PIECES[i][0] : PIECES[i][1]])
+
+        def load_x(tiles, src, g):
+            nc.sync.dma_start(out=tiles[g][:], in_=src[g])
+
+        def interleave(eng, dst, src):
+            if eng == "G":
+                nc.gpsimd.tensor_scalar(
+                    out=dst, in0=src.rearrange("p j c -> p c j"), scalar1=1.0, scalar2=0.0, op0=ALU.mult, op1=ALU.add
+                )
+                return
+            o, s = dst.rearrange("p (c i) j -> p c j i", i=4), src.rearrange("p j (c i) -> p c j i", i=4)
+            if eng == "V":
+                nc.vector.tensor_copy(out=o, in_=s)
+            else:
+                nc.scalar.copy(out=o, in_=s)
+
+        def warm_up():
+            warm = sb.tile([P, 2], F32, name="warm")
+            nc.vector.memset(warm[:, 0:1], 0.0)
+            nc.scalar.activation(out=warm[:, 1:2], in_=warm[:, 0:1], func=ACT.Sigmoid)
+
+        def quantize(codes, scales, src):
+            nc.vector.quantize_mx(out=codes.bitcast(FP8X4), scales=scales, in_=src[:].rearrange("p c j -> p (c j)"))
+
+        def quantize_w(k):
+            quantize(w_codes[k][:], w_scales[k][:], w_bf[k])
+
+        def quantize_h(i):
+            cols = slice(PIECES[i][0], PIECES[i][1])
+            quantize(h_codes[:, cols], h_scales[:, cols], h_bf[i])
+
+        def product(bank, k, g, first, last):
+            rows = slice(ROWS * g, ROWS * (g + 1))
+            for c in range(first, last, N_MM):
+                cols = slice(c, c + N_MM)
+                nc.tensor.matmul_mx(
+                    out=bank[g][:, cols],
+                    lhsT=w_codes[k][rows, :].bitcast(FP8X4),
+                    lhsT_scale=w_scales[k][rows, :],
+                    rhs=h_codes[rows, cols].bitcast(FP8X4),
+                    rhs_scale=h_scales[rows, cols],
+                    start=True,
+                    stop=True,
+                )
+
+        def reset_sum(g, cols):
+            nc.vector.tensor_tensor(out=pre_r[g][:, cols], in0=bank_ru[g][:, cols], in1=xr_sb[g][:, cols], op=ALU.add)
+
+        def reset_gate(g, cols):
+            nc.scalar.activation(out=gate_r[g][:, cols], in_=pre_r[g][:, cols], func=ACT.Sigmoid)
+
+        def update_sum(g, cols):
+            nc.vector.tensor_tensor(out=pre_u[g][:, cols], in0=bank_ru[g][:, cols], in1=xu_sb[g][:, cols], op=ALU.add)
+
+        def update_gate(g, cols):
+            nc.scalar.activation(out=gate_u[g][:, cols], in_=pre_u[g][:, cols], func=ACT.Sigmoid)
+
+        def gate_product(g, cols):
+            nc.vector.scalar_tensor_tensor(
+                out=gated[g][:, cols], in0=bank_c[g][:, cols], scalar=bias[:, g, 0:1], in1=gate_r[g][:, cols],
+                op0=ALU.add, op1=ALU.mult,
+            )
+
+        def add_xc(eng, g, cols):
+            eng.tensor_tensor(out=pre_c[g][:, cols], in0=gated[g][:, cols], in1=xc_sb[g][:, cols], op=ALU.add)
+
+        def candidate(g, cols):
+            nc.scalar.activation(out=cand[g][:, cols], in_=pre_c[g][:, cols], func=ACT.Tanh)
+
+        def keep(eng, g, cols):
+            eng.tensor_tensor(out=kept[g][:, cols], in0=gate_u[g][:, cols], in1=hp_sb[g][:, cols], op=ALU.mult)
+
+        def renew(g, cols):
+            nc.vector.scalar_tensor_tensor(
+                out=fresh[g][:, cols], in0=gate_u[g][:, cols], scalar=1.0, in1=cand[g][:, cols],
+                op0=ALU.subtract, op1=ALU.mult,
+            )
+
+        def mix(eng, g, cols):
+            eng.tensor_tensor(out=y[g][:, cols], in0=kept[g][:, cols], in1=fresh[g][:, cols], op=ALU.subtract)
+
+        def store(g, cols):
+            nc.sync.dma_start(out=out[g][:, cols], in_=y[g][:, cols])
+
+        with nc.allow_non_contiguous_dma(reason="one bias a partition"):
+            nc.gpsimd.dma_start(out=bias[:, :, 0:1], in_=bc.rearrange("g m o -> m g o"))
+
+        warm_up()
+        load_w("r")
+        load_h(0)
+        load_h(2)
+        interleave('S', h_bf[0][:, 160:256, :], h_raw[0][:, :, 160:256])
+        load_h(1)
+        load_w("c")
+        interleave('G', w_bf["r"][:], w_raw["r"][:])
+        quantize_w("r")
+        interleave('V', h_bf[0][:, 0:160, :], h_raw[0][:, :, 0:160])
+        quantize_h(0)
+        product(bank_ru, "r", 2, 0, 256)
+        product(bank_ru, "r", 0, 0, 256)
+        product(bank_ru, "r", 3, 0, 256)
+        product(bank_ru, "r", 1, 0, 256)
+        load_x(xr_sb, xr, 0)
+        load_w("u")
+        interleave('V', h_bf[1][:, 0:128, :], h_raw[1][:, :, 0:128])
+        quantize_h(1)
+        product(bank_ru, "r", 1, 256, 384)
+        product(bank_ru, "r", 0, 256, 384)
+        load_x(xr_sb, xr, 1)
+        load_x(xc_sb, xc, 0)
+        load_x(xr_sb, xr, 2)
+        load_x(xu_sb, xu, 0)
+        interleave('S', h_bf[2][:, 0:128, :], h_raw[2][:, :, 0:128])
+        quantize_h(2)
+        product(bank_ru, "r", 0, 384, 512)
+        product(bank_ru, "r", 1, 384, 512)
+        interleave('S', w_bf["c"][:], w_raw["c"][:])
+        quantize_w("c")
+        product(bank_c, "c", 0, 0, 512)
+        product(bank_c, "c", 1, 0, 512)
+        interleave('S', w_bf["u"][:], w_raw["u"][:])
+        load_x(xc_sb, xc, 1)
+        load_x(xu_sb, xu, 1)
+        load_x(xr_sb, xr, 3)
+        reset_sum(0, LO)
+        reset_gate(0, LO)
+        reset_sum(0, HI)
+        reset_gate(0, HI)
+        reset_sum(1, ALL)
+        reset_gate(1, LO)
+        reset_gate(1, HI)
+        load_x(hp_sb, hp, 0)
+        quantize_w("u")
+        product(bank_ru, "u", 0, 0, 512)
+        product(bank_ru, "r", 3, 256, 384)
+        load_x(hp_sb, hp, 1)
+        load_x(xu_sb, xu, 3)
+        load_x(xu_sb, xu, 2)
+        gate_product(0, LO)
+        add_xc(nc.gpsimd, 0, LO)
+        candidate(0, LO)
+        gate_product(0, HI)
+        add_xc(nc.gpsimd, 0, HI)
+        candidate(0, HI)
+        reset_sum(2, LO)
+        product(bank_ru, "r", 2, 256, 384)
+        load_x(xc_sb, xc, 2)
+        load_x(hp_sb, hp, 2)
+        gate_product(1, LO)
+        gate_product(1, HI)
+        update_sum(0, ALL)
+        update_gate(0, ALL)
+        load_x(xc_sb, xc, 3)
+        product(bank_ru, "r", 2, 384, 512)
+        reset_sum(2, HI)
+        reset_gate(2, ALL)
+        product(bank_ru, "u", 1, 0, 512)
+        update_sum(1, ALL)
+        update_gate(1, ALL)
+        load_x(hp_sb, hp, 3)
+        product(bank_ru, "r", 3, 384, 512)
+        reset_sum(3, ALL)
+        product(bank_ru, "u", 3, 0, 512)
+        reset_gate(3, ALL)
+        renew(0, ALL)
+        add_xc(nc.gpsimd, 1, ALL)
+        candidate(1, HI)
+        candidate(1, LO)
+        keep(nc.vector, 0, ALL)
+        mix(nc.gpsimd, 0, ALL)
+        store(0, ALL)
+        keep(nc.vector, 1, ALL)
+        update_sum(3, LO)
+        update_gate(3, LO)
+        update_sum(3, HI)
+        update_gate(3, HI)
+        product(bank_c, "c", 2, 0, 512)
+        gate_product(2, LO)
+        gate_product(2, HI)
+        add_xc(nc.vector, 2, LO)
+        add_xc(nc.gpsimd, 2, HI)
+        product(bank_c, "c", 3, 0, 512)
+        gate_product(3, LO)
+        gate_product(3, HI)
+        add_xc(nc.vector, 3, LO)
+        add_xc(nc.vector, 3, HI)
+        renew(1, ALL)
+        mix(nc.gpsimd, 1, ALL)
+        candidate(3, LO)
+        keep(nc.vector, 3, ALL)
+        product(bank_ru, "u", 2, 0, 512)
+        update_sum(2, LO)
+        update_sum(2, HI)
+        candidate(3, HI)
+        renew(3, ALL)
+        candidate(2, ALL)
+        store(1, ALL)
+        update_gate(2, LO)
+        update_gate(2, HI)
+        renew(2, ALL)
+        mix(nc.vector, 3, ALL)
+        store(3, ALL)
+        keep(nc.vector, 2, ALL)
+        mix(nc.vector, 2, LO)
+        store(2, LO)
+        mix(nc.vector, 2, HI)
+        store(2, HI)

@@ -17,9 +17,8 @@ P = 128
 PACK = 4
 ROWS = D // PACK
 HALF = N // 2
-PIECES = [(0, 256), (256, 384), (384, 512)]
-N_MM = 128
-ALL, LO, HI = slice(0, N), slice(0, HALF), slice(HALF, N)
+WHOLE, LOW, HIGH = slice(0, N), slice(0, HALF), slice(HALF, N)
+H_SPLIT = 384
 
 
 def tile_rows_cell_gru_kernel(tc, h, wr, wu, wc, xr, xu, xc, hp, bc, out):
@@ -32,18 +31,19 @@ def tile_rows_cell_gru_kernel(tc, h, wr, wu, wc, xr, xu, xc, hp, bc, out):
         def per_head(name):
             return [sb.tile([P, N], F32, name="%s%d" % (name, g)) for g in range(G)]
 
-        weights = {"r": wr, "u": wu, "c": wc}
+        weights = {"r": wr, "c": wc, "u": wu}
         w_raw, w_bf, w_codes, w_scales = {}, {}, {}, {}
         for k in weights:
             w_raw[k] = sb.tile([P, PACK, M], F32, name="w_raw_" + k)
             w_bf[k] = sb.tile([P, M, PACK], BF16, name="w_bf_" + k, align_bytes=64)
             w_codes[k] = sb.tile([P, M], U32, name="w_codes_" + k, align_bytes=64)
             w_scales[k] = sb.tile([P, M], U8, name="w_scales_" + k, align_bytes=64)
-        h_raw = [sb.tile([P, PACK, b - a], F32, name="h_raw%d" % a) for a, b in PIECES]
-        h_bf = [sb.tile([P, b - a, PACK], BF16, name="h_bf%d" % a, align_bytes=64) for a, b in PIECES]
+        h_raw = sb.tile([P, PACK, N], F32)
+        h_bf = sb.tile([P, N, PACK], BF16, align_bytes=64)
         h_codes = sb.tile([P, N], U32, align_bytes=64)
         h_scales = sb.tile([P, N], U8, align_bytes=64)
         bias = sb.tile([P, G, 8], F32)
+        warm = sb.tile([P, 2], F32)
 
         xr_sb, xu_sb, xc_sb, hp_sb = per_head("xr"), per_head("xu"), per_head("xc"), per_head("hp")
         pre_r, gate_r = per_head("pre_r"), per_head("gate_r")
@@ -53,217 +53,116 @@ def tile_rows_cell_gru_kernel(tc, h, wr, wu, wc, xr, xu, xc, hp, bc, out):
         bank_ru = [ps.tile([M, N], F32, name="bank_ru%d" % g) for g in range(G)]
         bank_c = [ps.tile([M, N], F32, name="bank_c%d" % g) for g in range(G)]
 
-        h_view = h.rearrange("g (p j) n -> (g p) j n", j=PACK)
-
-        def load_w(k):
-            nc.sync.dma_start(out=w_raw[k][:], in_=weights[k].rearrange("g (p j) m -> (g p) j m", j=PACK))
-
-        def load_h(i):
-            nc.sync.dma_start(out=h_raw[i][:], in_=h_view[:, :, PIECES[i][0] : PIECES[i][1]])
-
-        def load_x(tiles, src, g):
-            nc.sync.dma_start(out=tiles[g][:], in_=src[g])
-
-        def interleave(eng, dst, src):
-            if eng == "G":
-                nc.gpsimd.tensor_scalar(
-                    out=dst, in0=src.rearrange("p j c -> p c j"), scalar1=1.0, scalar2=0.0, op0=ALU.mult, op1=ALU.add
-                )
-                return
-            o, s = dst.rearrange("p (c i) j -> p c j i", i=4), src.rearrange("p j (c i) -> p c j i", i=4)
-            if eng == "V":
-                nc.vector.tensor_copy(out=o, in_=s)
-            else:
-                nc.scalar.copy(out=o, in_=s)
-
-        def warm_up():
-            warm = sb.tile([P, 2], F32, name="warm")
-            nc.vector.memset(warm[:, 0:1], 0.0)
-            nc.scalar.activation(out=warm[:, 1:2], in_=warm[:, 0:1], func=ACT.Sigmoid)
+        def interleave(copy, dst, src):
+            copy(out=dst.rearrange("p (c i) j -> p c j i", i=4), in_=src.rearrange("p j (c i) -> p c j i", i=4))
 
         def quantize(codes, scales, src):
-            nc.vector.quantize_mx(out=codes.bitcast(FP8X4), scales=scales, in_=src[:].rearrange("p c j -> p (c j)"))
+            nc.vector.quantize_mx(out=codes.bitcast(FP8X4), scales=scales, in_=src.rearrange("p c j -> p (c j)"))
 
-        def quantize_w(k):
-            quantize(w_codes[k][:], w_scales[k][:], w_bf[k])
-
-        def quantize_h(i):
-            cols = slice(PIECES[i][0], PIECES[i][1])
-            quantize(h_codes[:, cols], h_scales[:, cols], h_bf[i])
-
-        def product(bank, k, g, first, last):
+        def product(k, g):
             rows = slice(ROWS * g, ROWS * (g + 1))
-            for c in range(first, last, N_MM):
-                cols = slice(c, c + N_MM)
-                nc.tensor.matmul_mx(
-                    out=bank[g][:, cols],
-                    lhsT=w_codes[k][rows, :].bitcast(FP8X4),
-                    lhsT_scale=w_scales[k][rows, :],
-                    rhs=h_codes[rows, cols].bitcast(FP8X4),
-                    rhs_scale=h_scales[rows, cols],
-                    start=True,
-                    stop=True,
-                )
+            nc.tensor.matmul_mx(
+                out=(bank_c if k == "c" else bank_ru)[g][:],
+                lhsT=w_codes[k][rows, :].bitcast(FP8X4),
+                lhsT_scale=w_scales[k][rows, :],
+                rhs=h_codes[rows, :].bitcast(FP8X4),
+                rhs_scale=h_scales[rows, :],
+                start=True,
+                stop=True,
+            )
 
-        def reset_sum(g, cols):
+        def reset_gate(g, cols=WHOLE):
             nc.vector.tensor_tensor(out=pre_r[g][:, cols], in0=bank_ru[g][:, cols], in1=xr_sb[g][:, cols], op=ALU.add)
-
-        def reset_gate(g, cols):
             nc.scalar.activation(out=gate_r[g][:, cols], in_=pre_r[g][:, cols], func=ACT.Sigmoid)
 
-        def update_sum(g, cols):
-            nc.vector.tensor_tensor(out=pre_u[g][:, cols], in0=bank_ru[g][:, cols], in1=xu_sb[g][:, cols], op=ALU.add)
+        def update_gate(g):
+            nc.vector.tensor_tensor(out=pre_u[g][:], in0=bank_ru[g][:], in1=xu_sb[g][:], op=ALU.add)
+            nc.scalar.activation(out=gate_u[g][:], in_=pre_u[g][:], func=ACT.Sigmoid)
 
-        def update_gate(g, cols):
-            nc.scalar.activation(out=gate_u[g][:, cols], in_=pre_u[g][:, cols], func=ACT.Sigmoid)
-
-        def gate_product(g, cols):
+        def candidate_sum(g, cols=WHOLE):
             nc.vector.scalar_tensor_tensor(
                 out=gated[g][:, cols], in0=bank_c[g][:, cols], scalar=bias[:, g, 0:1], in1=gate_r[g][:, cols],
                 op0=ALU.add, op1=ALU.mult,
             )
+            nc.gpsimd.tensor_tensor(out=pre_c[g][:, cols], in0=gated[g][:, cols], in1=xc_sb[g][:, cols], op=ALU.add)
 
-        def add_xc(eng, g, cols):
-            eng.tensor_tensor(out=pre_c[g][:, cols], in0=gated[g][:, cols], in1=xc_sb[g][:, cols], op=ALU.add)
+        def candidate(g):
+            nc.scalar.activation(out=cand[g][:], in_=pre_c[g][:], func=ACT.Tanh)
 
-        def candidate(g, cols):
-            nc.scalar.activation(out=cand[g][:, cols], in_=pre_c[g][:, cols], func=ACT.Tanh)
+        def keep(g, cols=WHOLE):
+            nc.vector.tensor_tensor(out=kept[g][:, cols], in0=gate_u[g][:, cols], in1=hp_sb[g][:, cols], op=ALU.mult)
 
-        def keep(eng, g, cols):
-            eng.tensor_tensor(out=kept[g][:, cols], in0=gate_u[g][:, cols], in1=hp_sb[g][:, cols], op=ALU.mult)
-
-        def renew(g, cols):
+        def renew(g):
             nc.vector.scalar_tensor_tensor(
-                out=fresh[g][:, cols], in0=gate_u[g][:, cols], scalar=1.0, in1=cand[g][:, cols],
-                op0=ALU.subtract, op1=ALU.mult,
+                out=fresh[g][:], in0=gate_u[g][:], scalar=1.0, in1=cand[g][:], op0=ALU.subtract, op1=ALU.mult
             )
 
-        def mix(eng, g, cols):
-            eng.tensor_tensor(out=y[g][:, cols], in0=kept[g][:, cols], in1=fresh[g][:, cols], op=ALU.subtract)
-
-        def store(g, cols):
+        def mix(g, cols=WHOLE):
+            nc.vector.tensor_tensor(out=y[g][:, cols], in0=kept[g][:, cols], in1=fresh[g][:, cols], op=ALU.subtract)
             nc.sync.dma_start(out=out[g][:, cols], in_=y[g][:, cols])
 
         with nc.allow_non_contiguous_dma(reason="one bias a partition"):
             nc.gpsimd.dma_start(out=bias[:, :, 0:1], in_=bc.rearrange("g m o -> m g o"))
+        nc.vector.memset(warm[:, 0:1], 0.0)
+        nc.scalar.activation(out=warm[:, 1:2], in_=warm[:, 0:1], func=ACT.Sigmoid)
 
-        warm_up()
-        load_w("r")
-        load_h(0)
-        load_h(2)
-        interleave('S', h_bf[0][:, 160:256, :], h_raw[0][:, :, 160:256])
-        load_h(1)
-        load_w("c")
-        interleave('G', w_bf["r"][:], w_raw["r"][:])
-        quantize_w("r")
-        interleave('V', h_bf[0][:, 0:160, :], h_raw[0][:, :, 0:160])
-        quantize_h(0)
-        product(bank_ru, "r", 2, 0, 256)
-        product(bank_ru, "r", 0, 0, 256)
-        product(bank_ru, "r", 3, 0, 256)
-        product(bank_ru, "r", 1, 0, 256)
-        load_x(xr_sb, xr, 0)
-        load_w("u")
-        interleave('V', h_bf[1][:, 0:128, :], h_raw[1][:, :, 0:128])
-        quantize_h(1)
-        product(bank_ru, "r", 1, 256, 384)
-        product(bank_ru, "r", 0, 256, 384)
-        load_x(xr_sb, xr, 1)
-        load_x(xc_sb, xc, 0)
-        load_x(xr_sb, xr, 2)
-        load_x(xu_sb, xu, 0)
-        interleave('S', h_bf[2][:, 0:128, :], h_raw[2][:, :, 0:128])
-        quantize_h(2)
-        product(bank_ru, "r", 0, 384, 512)
-        product(bank_ru, "r", 1, 384, 512)
-        interleave('S', w_bf["c"][:], w_raw["c"][:])
-        quantize_w("c")
-        product(bank_c, "c", 0, 0, 512)
-        product(bank_c, "c", 1, 0, 512)
-        interleave('S', w_bf["u"][:], w_raw["u"][:])
-        load_x(xc_sb, xc, 1)
-        load_x(xu_sb, xu, 1)
-        load_x(xr_sb, xr, 3)
-        reset_sum(0, LO)
-        reset_gate(0, LO)
-        reset_sum(0, HI)
-        reset_gate(0, HI)
-        reset_sum(1, ALL)
-        reset_gate(1, LO)
-        reset_gate(1, HI)
-        load_x(hp_sb, hp, 0)
-        quantize_w("u")
-        product(bank_ru, "u", 0, 0, 512)
-        product(bank_ru, "r", 3, 256, 384)
-        load_x(hp_sb, hp, 1)
-        load_x(xu_sb, xu, 3)
-        load_x(xu_sb, xu, 2)
-        gate_product(0, LO)
-        add_xc(nc.gpsimd, 0, LO)
-        candidate(0, LO)
-        gate_product(0, HI)
-        add_xc(nc.gpsimd, 0, HI)
-        candidate(0, HI)
-        reset_sum(2, LO)
-        product(bank_ru, "r", 2, 256, 384)
-        load_x(xc_sb, xc, 2)
-        load_x(hp_sb, hp, 2)
-        gate_product(1, LO)
-        gate_product(1, HI)
-        update_sum(0, ALL)
-        update_gate(0, ALL)
-        load_x(xc_sb, xc, 3)
-        product(bank_ru, "r", 2, 384, 512)
-        reset_sum(2, HI)
-        reset_gate(2, ALL)
-        product(bank_ru, "u", 1, 0, 512)
-        update_sum(1, ALL)
-        update_gate(1, ALL)
-        load_x(hp_sb, hp, 3)
-        product(bank_ru, "r", 3, 384, 512)
-        reset_sum(3, ALL)
-        product(bank_ru, "u", 3, 0, 512)
-        reset_gate(3, ALL)
-        renew(0, ALL)
-        add_xc(nc.gpsimd, 1, ALL)
-        candidate(1, HI)
-        candidate(1, LO)
-        keep(nc.vector, 0, ALL)
-        mix(nc.gpsimd, 0, ALL)
-        store(0, ALL)
-        keep(nc.vector, 1, ALL)
-        update_sum(3, LO)
-        update_gate(3, LO)
-        update_sum(3, HI)
-        update_gate(3, HI)
-        product(bank_c, "c", 2, 0, 512)
-        gate_product(2, LO)
-        gate_product(2, HI)
-        add_xc(nc.vector, 2, LO)
-        add_xc(nc.gpsimd, 2, HI)
-        product(bank_c, "c", 3, 0, 512)
-        gate_product(3, LO)
-        gate_product(3, HI)
-        add_xc(nc.vector, 3, LO)
-        add_xc(nc.vector, 3, HI)
-        renew(1, ALL)
-        mix(nc.gpsimd, 1, ALL)
-        candidate(3, LO)
-        keep(nc.vector, 3, ALL)
-        product(bank_ru, "u", 2, 0, 512)
-        update_sum(2, LO)
-        update_sum(2, HI)
-        candidate(3, HI)
-        renew(3, ALL)
-        candidate(2, ALL)
-        store(1, ALL)
-        update_gate(2, LO)
-        update_gate(2, HI)
-        renew(2, ALL)
-        mix(nc.vector, 3, ALL)
-        store(3, ALL)
-        keep(nc.vector, 2, ALL)
-        mix(nc.vector, 2, LO)
-        store(2, LO)
-        mix(nc.vector, 2, HI)
-        store(2, HI)
+        nc.sync.dma_start(out=h_raw[:], in_=h.rearrange("g (p j) n -> (g p) j n", j=PACK))
+        for k in weights:
+            nc.sync.dma_start(out=w_raw[k][:], in_=weights[k].rearrange("g (p j) m -> (g p) j m", j=PACK))
+        for tiles, src, g in [
+            (xr_sb, xr, 0), (xr_sb, xr, 1), (xc_sb, xc, 0), (xr_sb, xr, 2), (xc_sb, xc, 1), (xr_sb, xr, 3),
+            (xu_sb, xu, 0), (xc_sb, xc, 2), (xc_sb, xc, 3), (xu_sb, xu, 1), (xu_sb, xu, 2), (xu_sb, xu, 3),
+            (hp_sb, hp, 0), (hp_sb, hp, 1), (hp_sb, hp, 2), (hp_sb, hp, 3),
+        ]:
+            nc.sync.dma_start(out=tiles[g][:], in_=src[g])
+
+        interleave(nc.vector.tensor_copy, h_bf[:, :HALF, :], h_raw[:, :, :HALF])
+        interleave(nc.vector.tensor_copy, h_bf[:, HALF:H_SPLIT, :], h_raw[:, :, HALF:H_SPLIT])
+        interleave(nc.scalar.copy, h_bf[:, H_SPLIT:, :], h_raw[:, :, H_SPLIT:])
+        for cols in (LOW, HIGH):
+            quantize(h_codes[:, cols], h_scales[:, cols], h_bf[:, cols, :])
+        for k in weights:
+            interleave(nc.scalar.copy, w_bf[k][:], w_raw[k][:])
+            quantize(w_codes[k][:], w_scales[k][:], w_bf[k][:])
+
+        product("r", 0)
+        product("r", 1)
+        product("c", 0)
+        product("r", 2)
+        product("c", 1)
+        product("r", 3)
+        product("c", 2)
+        product("c", 3)
+
+        reset_gate(0, LOW)
+        reset_gate(0, HIGH)
+        product("u", 0)
+        reset_gate(1)
+        product("u", 1)
+        candidate_sum(0, LOW)
+        candidate_sum(0, HIGH)
+        reset_gate(2)
+        product("u", 2)
+        candidate_sum(1)
+        reset_gate(3)
+        product("u", 3)
+        candidate_sum(2)
+        candidate(0)
+        update_gate(0)
+        candidate_sum(3)
+        candidate(1)
+        update_gate(1)
+        update_gate(2)
+        candidate(2)
+        update_gate(3)
+        candidate(3)
+
+        renew(0)
+        for g in range(G - 1):
+            keep(g)
+            renew(g + 1)
+            mix(g)
+        keep(G - 1, LOW)
+        keep(G - 1, HIGH)
+        mix(G - 1, LOW)
+        mix(G - 1, HIGH)

@@ -42,10 +42,14 @@ def tile_rows_cell_gru_kernel(tc, h, wr, wu, wc, xr, xu, xc, hp, bc, out):
         h_bf = sb.tile([P, N, PACK], BF16, align_bytes=64)
         h_codes = sb.tile([P, N], U32, align_bytes=64)
         h_scales = sb.tile([P, N], U8, align_bytes=64)
-        bias = sb.tile([P, G, 8], F32)
+        bias_rows = sb.tile([P, G * ROWS], F32, align_bytes=64)
+        bias = sb.tile([P, G * ROWS], F32, align_bytes=64)
         warm = sb.tile([P, 2], F32)
 
-        xr_sb, xu_sb, xc_sb, hp_sb = per_head("xr"), per_head("xu"), per_head("xc"), per_head("hp")
+        xr_sb = sb.tile([P, G, N], F32)
+        xu_sb = sb.tile([P, G, N], F32)
+        xc_sb = sb.tile([P, G, N], F32)
+        hp_sb = sb.tile([P, G, N], F32)
         pre_r, gate_r = per_head("pre_r"), per_head("gate_r")
         pre_u, gate_u = per_head("pre_u"), per_head("gate_u")
         gated, pre_c, cand = per_head("gated"), per_head("pre_c"), per_head("cand")
@@ -72,25 +76,25 @@ def tile_rows_cell_gru_kernel(tc, h, wr, wu, wc, xr, xu, xc, hp, bc, out):
             )
 
         def reset_gate(g, cols=WHOLE):
-            nc.vector.tensor_tensor(out=pre_r[g][:, cols], in0=bank_ru[g][:, cols], in1=xr_sb[g][:, cols], op=ALU.add)
+            nc.vector.tensor_tensor(out=pre_r[g][:, cols], in0=bank_ru[g][:, cols], in1=xr_sb[:, g, cols], op=ALU.add)
             nc.scalar.activation(out=gate_r[g][:, cols], in_=pre_r[g][:, cols], func=ACT.Sigmoid)
 
         def update_gate(g):
-            nc.vector.tensor_tensor(out=pre_u[g][:], in0=bank_ru[g][:], in1=xu_sb[g][:], op=ALU.add)
+            nc.vector.tensor_tensor(out=pre_u[g][:], in0=bank_ru[g][:], in1=xu_sb[:, g, :], op=ALU.add)
             nc.scalar.activation(out=gate_u[g][:], in_=pre_u[g][:], func=ACT.Sigmoid)
 
         def candidate_sum(g, cols=WHOLE):
             nc.vector.scalar_tensor_tensor(
-                out=gated[g][:, cols], in0=bank_c[g][:, cols], scalar=bias[:, g, 0:1], in1=gate_r[g][:, cols],
+                out=gated[g][:, cols], in0=bank_c[g][:, cols], scalar=bias[:, ROWS * g : ROWS * g + 1], in1=gate_r[g][:, cols],
                 op0=ALU.add, op1=ALU.mult,
             )
-            nc.gpsimd.tensor_tensor(out=pre_c[g][:, cols], in0=gated[g][:, cols], in1=xc_sb[g][:, cols], op=ALU.add)
+            nc.gpsimd.tensor_tensor(out=pre_c[g][:, cols], in0=gated[g][:, cols], in1=xc_sb[:, g, cols], op=ALU.add)
 
         def candidate(g):
             nc.scalar.activation(out=cand[g][:], in_=pre_c[g][:], func=ACT.Tanh)
 
         def keep(g, cols=WHOLE):
-            nc.vector.tensor_tensor(out=kept[g][:, cols], in0=gate_u[g][:, cols], in1=hp_sb[g][:, cols], op=ALU.mult)
+            nc.vector.tensor_tensor(out=kept[g][:, cols], in0=gate_u[g][:, cols], in1=hp_sb[:, g, cols], op=ALU.mult)
 
         def renew(g):
             nc.vector.scalar_tensor_tensor(
@@ -101,20 +105,21 @@ def tile_rows_cell_gru_kernel(tc, h, wr, wu, wc, xr, xu, xc, hp, bc, out):
             nc.vector.tensor_tensor(out=y[g][:, cols], in0=kept[g][:, cols], in1=fresh[g][:, cols], op=ALU.subtract)
             nc.sync.dma_start(out=out[g][:, cols], in_=y[g][:, cols])
 
-        with nc.allow_non_contiguous_dma(reason="one bias a partition"):
-            nc.gpsimd.dma_start(out=bias[:, :, 0:1], in_=bc.rearrange("g m o -> m g o"))
+        nc.gpsimd.memset(bias_rows[:], 0.0)
+        nc.scalar.dma_start(
+            out=bias_rows[0:P:ROWS, :].rearrange("b (g i) -> b g i", g=G), in_=bc.rearrange("g (b i) o -> b g (i o)", i=ROWS)
+        )
         nc.vector.memset(warm[:, 0:1], 0.0)
         nc.scalar.activation(out=warm[:, 1:2], in_=warm[:, 0:1], func=ACT.Sigmoid)
 
         nc.sync.dma_start(out=h_raw[:], in_=h.rearrange("g (p j) n -> (g p) j n", j=PACK))
         for k in weights:
             nc.sync.dma_start(out=w_raw[k][:], in_=weights[k].rearrange("g (p j) m -> (g p) j m", j=PACK))
-        for tiles, src, g in [
-            (xr_sb, xr, 0), (xr_sb, xr, 1), (xc_sb, xc, 0), (xr_sb, xr, 2), (xc_sb, xc, 1), (xr_sb, xr, 3),
-            (xu_sb, xu, 0), (xc_sb, xc, 2), (xc_sb, xc, 3), (xu_sb, xu, 1), (xu_sb, xu, 2), (xu_sb, xu, 3),
-            (hp_sb, hp, 0), (hp_sb, hp, 1), (hp_sb, hp, 2), (hp_sb, hp, 3),
+        for tile, src, first, last in [
+            (xr_sb, xr, 0, 2), (xc_sb, xc, 0, 1), (xr_sb, xr, 2, 4), (xc_sb, xc, 1, 3), (xu_sb, xu, 0, 1),
+            (xu_sb, xu, 1, 3), (xc_sb, xc, 3, 4), (xu_sb, xu, 3, 4), (hp_sb, hp, 0, 1), (hp_sb, hp, 1, 4),
         ]:
-            nc.sync.dma_start(out=tiles[g][:], in_=src[g])
+            nc.sync.dma_start(out=tile[:, first:last, :], in_=src[first:last].rearrange("g m n -> m g n"))
 
         interleave(nc.vector.tensor_copy, h_bf[:, :HALF, :], h_raw[:, :, :HALF])
         interleave(nc.vector.tensor_copy, h_bf[:, HALF:H_SPLIT, :], h_raw[:, :, HALF:H_SPLIT])
@@ -124,6 +129,8 @@ def tile_rows_cell_gru_kernel(tc, h, wr, wu, wc, xr, xu, xc, hp, bc, out):
         for k in weights:
             interleave(nc.scalar.copy, w_bf[k][:], w_raw[k][:])
             quantize(w_codes[k][:], w_scales[k][:], w_bf[k][:])
+            if k == "r":
+                nc.vector.transpose(bias[:], bias_rows[:])
 
         product("r", 0)
         product("r", 1)

@@ -19,6 +19,7 @@ ROWS = D // PACK
 HALF = N // 2
 WHOLE, LOW, HIGH = slice(0, N), slice(0, HALF), slice(HALF, N)
 H_SPLIT = 384
+LAST_SPLIT = 128
 
 
 def tile_rows_cell_gru_kernel(tc, h, wr, wu, wc, xr, xu, xc, hp, bc, out):
@@ -88,7 +89,9 @@ def tile_rows_cell_gru_kernel(tc, h, wr, wu, wc, xr, xu, xc, hp, bc, out):
                 out=gated[g][:, cols], in0=bank_c[g][:, cols], scalar=bias[:, ROWS * g : ROWS * g + 1], in1=gate_r[g][:, cols],
                 op0=ALU.add, op1=ALU.mult,
             )
-            nc.gpsimd.tensor_tensor(out=pre_c[g][:, cols], in0=gated[g][:, cols], in1=xc_sb[:, g, cols], op=ALU.add)
+
+        def add_xc(engine, g, cols=WHOLE):
+            engine.tensor_tensor(out=pre_c[g][:, cols], in0=gated[g][:, cols], in1=xc_sb[:, g, cols], op=ALU.add)
 
         def candidate(g):
             nc.scalar.activation(out=cand[g][:], in_=pre_c[g][:], func=ACT.Tanh)
@@ -147,21 +150,27 @@ def tile_rows_cell_gru_kernel(tc, h, wr, wu, wc, xr, xu, xc, hp, bc, out):
         reset_gate(1)
         product("u", 1)
         candidate_sum(0, LOW)
+        add_xc(nc.gpsimd, 0, LOW)
         candidate_sum(0, HIGH)
+        add_xc(nc.gpsimd, 0, HIGH)
         reset_gate(2)
         product("u", 2)
         candidate_sum(1)
+        add_xc(nc.gpsimd, 1)
         reset_gate(3)
         product("u", 3)
         candidate_sum(2)
+        add_xc(nc.gpsimd, 2)
         candidate(0)
         update_gate(0)
         candidate_sum(3)
+        add_xc(nc.gpsimd, 3, slice(0, LAST_SPLIT))
         candidate(1)
         update_gate(1)
         update_gate(2)
         candidate(2)
         update_gate(3)
+        add_xc(nc.vector, 3, slice(LAST_SPLIT, N))
         candidate(3)
 
         renew(0)

from contextlib import ExitStack

import concourse.mybir as mybir

G, D, M, N = 4, 128, 128, 512
FLOPS = 3 * 2 * G * D * M * N

F32 = mybir.dt.float32
BF16 = mybir.dt.bfloat16
U32 = mybir.dt.uint32
U8 = mybir.dt.uint8
FP8X4 = mybir.dt.float8_e4m3fn_x4
ALU = mybir.AluOpType
ACT = mybir.ActivationFunctionType

P = 128
PACK = 4
ROWS = D // PACK
HALF = N // 2
WHOLE, LOW, HIGH = slice(0, N), slice(0, HALF), slice(HALF, N)
H_SPLIT = 384
LAST_SPLIT = 128


def tile_rows_cell_gru_kernel(tc, h, wr, wu, wc, xr, xu, xc, hp, bc, out):
    nc = tc.nc
    with ExitStack() as ctx:
        sb = ctx.enter_context(tc.tile_pool(name="sb", bufs=1))
        ps = ctx.enter_context(tc.psum_pool(name="ps", bufs=1))
        ctx.enter_context(tc.manual_schedule())

        def per_head(name):
            return [sb.tile([P, N], F32, name="%s%d" % (name, g)) for g in range(G)]

        weights = {"r": wr, "c": wc, "u": wu}
        w_raw, w_bf, w_codes, w_scales = {}, {}, {}, {}
        for k in weights:
            w_raw[k] = sb.tile([P, PACK, M], F32, name="w_raw_" + k)
            w_bf[k] = sb.tile([P, M, PACK], BF16, name="w_bf_" + k, align_bytes=64)
            w_codes[k] = sb.tile([P, M], U32, name="w_codes_" + k, align_bytes=64)
            w_scales[k] = sb.tile([P, M], U8, name="w_scales_" + k, align_bytes=64)
        h_raw = sb.tile([P, PACK, N], F32)
        h_bf = sb.tile([P, N, PACK], BF16, align_bytes=64)
        h_codes = sb.tile([P, N], U32, align_bytes=64)
        h_scales = sb.tile([P, N], U8, align_bytes=64)
        bias_rows = sb.tile([P, G * ROWS], F32, align_bytes=64)
        bias = sb.tile([P, G * ROWS], F32, align_bytes=64)
        warm = sb.tile([P, 2], F32)

        xr_sb = sb.tile([P, G, N], F32)
        xu_sb = sb.tile([P, G, N], F32)
        xc_sb = sb.tile([P, G, N], F32)
        hp_sb = sb.tile([P, G, N], F32)
        pre_r, gate_r = per_head("pre_r"), per_head("gate_r")
        pre_u, gate_u = per_head("pre_u"), per_head("gate_u")
        gated, pre_c, cand = per_head("gated"), per_head("pre_c"), per_head("cand")
        kept, fresh, y = per_head("kept"), per_head("fresh"), per_head("y")
        bank_ru = [ps.tile([M, N], F32, name="bank_ru%d" % g) for g in range(G)]
        bank_c = [ps.tile([M, N], F32, name="bank_c%d" % g) for g in range(G)]

        def interleave(copy, dst, src):
            copy(out=dst.rearrange("p (c i) j -> p c j i", i=4), in_=src.rearrange("p j (c i) -> p c j i", i=4))

        def quantize(codes, scales, src):
            nc.vector.quantize_mx(out=codes.bitcast(FP8X4), scales=scales, in_=src.rearrange("p c j -> p (c j)"))

        def product(k, g):
            rows = slice(ROWS * g, ROWS * (g + 1))
            nc.tensor.matmul_mx(
                out=(bank_c if k == "c" else bank_ru)[g][:],
                lhsT=w_codes[k][rows, :].bitcast(FP8X4),
                lhsT_scale=w_scales[k][rows, :],
                rhs=h_codes[rows, :].bitcast(FP8X4),
                rhs_scale=h_scales[rows, :],
                start=True,
                stop=True,
            )

        def reset_gate(g, cols=WHOLE):
            nc.vector.tensor_tensor(out=pre_r[g][:, cols], in0=bank_ru[g][:, cols], in1=xr_sb[:, g, cols], op=ALU.add)
            nc.scalar.activation(out=gate_r[g][:, cols], in_=pre_r[g][:, cols], func=ACT.Sigmoid)

        def update_gate(g):
            nc.vector.tensor_tensor(out=pre_u[g][:], in0=bank_ru[g][:], in1=xu_sb[:, g, :], op=ALU.add)
            nc.scalar.activation(out=gate_u[g][:], in_=pre_u[g][:], func=ACT.Sigmoid)

        def candidate_sum(g, cols=WHOLE):
            nc.vector.scalar_tensor_tensor(
                out=gated[g][:, cols], in0=bank_c[g][:, cols], scalar=bias[:, ROWS * g : ROWS * g + 1], in1=gate_r[g][:, cols],
                op0=ALU.add, op1=ALU.mult,
            )

        def add_xc(engine, g, cols=WHOLE):
            engine.tensor_tensor(out=pre_c[g][:, cols], in0=gated[g][:, cols], in1=xc_sb[:, g, cols], op=ALU.add)

        def candidate(g):
            nc.scalar.activation(out=cand[g][:], in_=pre_c[g][:], func=ACT.Tanh)

        def keep(g, cols=WHOLE):
            nc.vector.tensor_tensor(out=kept[g][:, cols], in0=gate_u[g][:, cols], in1=hp_sb[:, g, cols], op=ALU.mult)

        def renew(g):
            nc.vector.scalar_tensor_tensor(
                out=fresh[g][:], in0=gate_u[g][:], scalar=1.0, in1=cand[g][:], op0=ALU.subtract, op1=ALU.mult
            )

        def mix(g, cols=WHOLE):
            nc.vector.tensor_tensor(out=y[g][:, cols], in0=kept[g][:, cols], in1=fresh[g][:, cols], op=ALU.subtract)
            nc.sync.dma_start(out=out[g][:, cols], in_=y[g][:, cols])

        nc.gpsimd.memset(bias_rows[:], 0.0)
        nc.scalar.dma_start(
            out=bias_rows[0:P:ROWS, :].rearrange("b (g i) -> b g i", g=G), in_=bc.rearrange("g (b i) o -> b g (i o)", i=ROWS)
        )
        nc.vector.memset(warm[:, 0:1], 0.0)
        nc.scalar.activation(out=warm[:, 1:2], in_=warm[:, 0:1], func=ACT.Sigmoid)

        nc.sync.dma_start(out=h_raw[:], in_=h.rearrange("g (p j) n -> (g p) j n", j=PACK))
        for k in weights:
            nc.sync.dma_start(out=w_raw[k][:], in_=weights[k].rearrange("g (p j) m -> (g p) j m", j=PACK))
        for tile, src, first, last in [
            (xr_sb, xr, 0, 2), (xc_sb, xc, 0, 1), (xr_sb, xr, 2, 4), (xc_sb, xc, 1, 3), (xu_sb, xu, 0, 1),
            (xu_sb, xu, 1, 3), (xc_sb, xc, 3, 4), (xu_sb, xu, 3, 4), (hp_sb, hp, 0, 1), (hp_sb, hp, 1, 4),
        ]:
            nc.sync.dma_start(out=tile[:, first:last, :], in_=src[first:last].rearrange("g m n -> m g n"))

        interleave(nc.vector.tensor_copy, h_bf[:, :HALF, :], h_raw[:, :, :HALF])
        interleave(nc.vector.tensor_copy, h_bf[:, HALF:H_SPLIT, :], h_raw[:, :, HALF:H_SPLIT])
        interleave(nc.scalar.copy, h_bf[:, H_SPLIT:, :], h_raw[:, :, H_SPLIT:])
        for cols in (LOW, HIGH):
            quantize(h_codes[:, cols], h_scales[:, cols], h_bf[:, cols, :])
        for k in weights:
            interleave(nc.scalar.copy, w_bf[k][:], w_raw[k][:])
            quantize(w_codes[k][:], w_scales[k][:], w_bf[k][:])
            if k == "r":
                nc.vector.transpose(bias[:], bias_rows[:])

        product("r", 0)
        product("r", 1)
        product("c", 0)
        product("r", 2)
        product("c", 1)
        product("r", 3)
        product("c", 2)
        product("c", 3)

        reset_gate(0, LOW)
        reset_gate(0, HIGH)
        product("u", 0)
        reset_gate(1)
        product("u", 1)
        candidate_sum(0, LOW)
        add_xc(nc.gpsimd, 0, LOW)
        candidate_sum(0, HIGH)
        add_xc(nc.gpsimd, 0, HIGH)
        reset_gate(2)
        product("u", 2)
        candidate_sum(1)
        add_xc(nc.gpsimd, 1)
        reset_gate(3)
        product("u", 3)
        candidate_sum(2)
        add_xc(nc.gpsimd, 2)
        candidate(0)
        update_gate(0)
        candidate_sum(3)
        add_xc(nc.gpsimd, 3, slice(0, LAST_SPLIT))
        candidate(1)
        update_gate(1)
        update_gate(2)
        candidate(2)
        update_gate(3)
        add_xc(nc.vector, 3, slice(LAST_SPLIT, N))
        candidate(3)

        renew(0)
        for g in range(G - 1):
            keep(g)
            renew(g + 1)
            mix(g)
        keep(G - 1, LOW)
        keep(G - 1, HIGH)
        mix(G - 1, LOW)
        mix(G - 1, HIGH)
